import numpy as np
import ml_dtypes


def mxq(x, axis, fmt="e4m3"):
    dtype, down = {"e4m3": (ml_dtypes.float8_e4m3fn, 7), "e5m2": (ml_dtypes.float8_e5m2, 14)}[fmt]
    v = np.moveaxis(np.asarray(x, np.float32).astype(ml_dtypes.bfloat16).astype(np.float64), axis, -1)
    blocks = v.reshape(v.shape[:-1] + (-1, 32))
    amax = np.abs(blocks).max(-1, keepdims=True)
    byte = np.maximum(np.where(amax > 0, np.frexp(amax)[1] - 1 + 127, 0) - down, 1)
    scale = np.exp2(byte - 127.0)
    codes = (blocks / scale).astype(np.float32).astype(dtype).astype(np.float64)
    return np.moveaxis((codes * scale).reshape(v.shape), -1, axis)


WIDE = False


def mx_kscale(k):
    if not WIDE:
        return np.ones(k)
    levels = np.array([10, -10, 5, -5, 0])
    if k % 512:
        return np.exp2(np.random.permutation(np.resize(levels, k // 32))).repeat(32)
    a = np.empty((k // 512, 16))
    for p in range(k // 512):
        a[p, :8] = np.random.permutation(np.resize(levels, 8))
        for g in range(8):
            far = levels[np.abs(levels - a[p, g]) >= 10]
            a[p, g + 8] = far[np.random.randint(len(far))]
    return np.exp2(a.ravel()).repeat(32)


def f64(x):
    return np.asarray(x).astype(np.float64)


E2M1 = np.array([0.0, 0.5, 1.0, 1.5, 2.0, 3.0, 4.0, 6.0, -0.0, -0.5, -1.0, -1.5, -2.0, -3.0, -4.0, -6.0])


def pack_weight(w, fmt):
    k, n = w.shape
    w = f64(np.asarray(w, np.float32).astype(ml_dtypes.bfloat16)).reshape(k // 32, 32, n)
    amax = np.abs(w).max(1)
    if fmt == "e4m3":
        byte = np.frexp(amax)[1] - 1 + 127 - 7
    else:
        mant, ex = np.frexp(amax / 6.0)
        byte = np.where(mant > 0.5, ex, ex - 1) + 127
    byte = np.clip(np.where(amax > 0, byte, 1), 1, 254)
    scaled = (w * np.exp2(127.0 - byte)[:, None, :]).reshape(k, n).astype(np.float32)
    by_word = np.ascontiguousarray(scaled.reshape(k // 512, 128, 4, n).transpose(0, 1, 3, 2))
    if fmt == "e4m3":
        words = by_word.astype(ml_dtypes.float8_e4m3fn).view(np.uint8)
    else:
        c = by_word.astype(ml_dtypes.float4_e2m1fn).view(np.uint8) & 0xF
        words = (c[..., 0::2] | (c[..., 1::2] << 4)).reshape(k // 512, 128, 2 * n)
    return np.ascontiguousarray(words), np.ascontiguousarray(byte.astype(np.uint8).reshape(k // 512, 16, n))


def unpack_weight(words, scales, fmt):
    g, _, n = scales.shape
    words = np.ascontiguousarray(words).reshape(g, 128, n, -1)
    if fmt == "e4m3":
        vals = words.view(ml_dtypes.float8_e4m3fn).astype(np.float64)
    else:
        nib = np.empty((g, 128, n, 4), np.uint8)
        nib[..., 0::2] = words & 0xF
        nib[..., 1::2] = words >> 4
        vals = E2M1[nib]
    vals = vals * np.repeat(np.exp2(scales.astype(np.float64) - 127.0), 8, axis=1)[..., None]
    return vals.transpose(0, 1, 3, 2).reshape(g * 512, n)


O, K, M, T = 512, 2048, 512, 512


def setup_inputs():
    n = np.random.standard_normal
    s = mx_kscale(K)[:, None]
    x = n((K, T)); x[:O] *= 6.0
    w = n((K, M)) / np.sqrt(K) / s; w[:O] /= 2.0
    p_x4 = pack_weight(x[O:] * s[O:], "e2m1")
    p_w4 = pack_weight(w[O:], "e2m1")
    return {
        "x8": (x[:O] * s[:O]).astype(np.float32),
        "w8": (w[:O]).astype(np.float32),
        "x4_words": p_x4[0],
        "x4_scales": p_x4[1],
        "w4_words": p_w4[0],
        "w4_scales": p_w4[1],
    }


def reference(x8, w8, x4_words, x4_scales, w4_words, w4_scales):
    x8_ = mxq(f64(x8), 0, "e4m3")
    w8_ = mxq(f64(w8), 0, "e4m3")
    x4_ = unpack_weight(x4_words, x4_scales, "e2m1")
    w4_ = unpack_weight(w4_words, w4_scales, "e2m1")
    y = w8_.T @ x8_ + w4_.T @ x4_
    return y

from contextlib import ExitStack

import concourse.mybir as mybir

O, K4, M, T = 512, 1536, 512, 512
FLOPS = 2 * M * T * (O + K4)

F32 = mybir.dt.float32
BF16 = mybir.dt.bfloat16
U32 = mybir.dt.uint32
I32 = mybir.dt.int32
U8 = mybir.dt.uint8
FP8X4 = mybir.dt.float8_e4m3fn_x4
FP4X4 = mybir.dt.float4_e2m1fn_x4

P = 128
PASSES4 = K4 // 512


def tile_mix_atom_fm_none_kernel(tc, x8, w8, x4_words, x4_scales, w4_words, w4_scales, out):
    nc = tc.nc
    with ExitStack() as ctx:
        keep = ctx.enter_context(tc.tile_pool(name="keep", bufs=1))
        psum = ctx.enter_context(tc.psum_pool(name="psum", bufs=1))
        ctx.enter_context(tc.manual_schedule())

        x4w = keep.tile([P, PASSES4 * 2 * T], U8, align_bytes=64, name="x4w")
        w4w = keep.tile([P, PASSES4 * 2 * M], U8, align_bytes=64, name="w4w")
        x4s = keep.tile([P, PASSES4 * T], U8, align_bytes=64, name="x4s")
        w4s = keep.tile([P, PASSES4 * M], U8, align_bytes=64, name="w4s")
        x_raw = keep.tile([P, 4, T], F32, align_bytes=64, name="x_raw")
        w_raw = [keep.tile([P, 4, 256], F32, align_bytes=64, name="w_raw%d" % h) for h in range(2)]

        def memset0(tile):
            nc.vector.memset(tile[:].bitcast(I32), 0)

        warm_in = keep.tile([P, 1024], BF16, align_bytes=64, name="warm_in")
        warm_codes = keep.tile([P, 256], U32, align_bytes=64, name="warm_codes")
        warm_planes = keep.tile([P, 256], U8, align_bytes=64, name="warm_planes")
        junk = psum.tile([P, 256], F32, name="junk")
        memset0(x4s)
        memset0(warm_in)
        memset0(w4s)
        nc.vector.quantize_mx(out=warm_codes[:].bitcast(FP8X4), scales=warm_planes[:], in_=warm_in[:])
        for i in range(12):
            nc.tensor.matmul_mx(
                out=junk[:],
                lhsT=warm_codes[:, 0:128].bitcast(FP8X4),
                lhsT_scale=warm_planes[:, 0:128],
                rhs=warm_codes[:].bitcast(FP8X4),
                rhs_scale=warm_planes[:],
                start=True,
                stop=True,
            )
        w8_rows = w8.rearrange("(p j) n -> p j n", j=4)
        x4s_rows = x4_scales.bitcast(I32).rearrange("a q n -> q a n")
        w4s_rows = w4_scales.bitcast(I32).rearrange("a q n -> q a n")

        def words(queue, tile, src):
            queue.dma_start(out=tile[:].bitcast(I32).rearrange("p (a c) -> p a c", a=PASSES4), in_=src.bitcast(I32).rearrange("a p c -> p a c"))

        def scale_rows(queue, plane, rows, q):
            queue.dma_start(out=plane[32 * q : 32 * q + 4, :].bitcast(I32).rearrange("p (a n) -> p a n", a=PASSES4), in_=rows[4 * q : 4 * q + 4])

        words(nc.sync, x4w, x4_words)
        words(nc.gpsimd, w4w, w4_words)
        scale_rows(nc.sync, x4s, x4s_rows, 0)
        scale_rows(nc.sync, x4s, x4s_rows, 1)
        scale_rows(nc.sync, x4s, x4s_rows, 2)
        scale_rows(nc.sync, x4s, x4s_rows, 3)
        scale_rows(nc.sync, w4s, w4s_rows, 0)
        scale_rows(nc.sync, w4s, w4s_rows, 1)
        scale_rows(nc.sync, w4s, w4s_rows, 2)
        scale_rows(nc.sync, w4s, w4s_rows, 3)
        nc.gpsimd.dma_start(out=x_raw[:], in_=x8.rearrange("(p j) t -> p j t", j=4))
        nc.gpsimd.dma_start(out=w_raw[0][:], in_=w8_rows[:, :, 0:256])
        nc.gpsimd.dma_start(out=w_raw[1][:], in_=w8_rows[:, :, 256:512])

        warm = keep.tile([P, 8], F32, name="warm")
        nc.vector.memset(warm[:], 0.0)
        nc.scalar.copy(warm[:, 4:5], warm[:, 0:1])

        acc = {}
        for m in range(4):
            for t0, n in ([(0, 512)] if m < 2 else [(0, 256), (256, 256)]):
                acc[m, t0] = (psum.tile([P, n], F32, name="acc%d_%d" % (m, t0)), n)

        for (m, t0), (bank, n) in acc.items():
            for a in range(PASSES4):
                nc.tensor.matmul_mx(
                    out=bank[:],
                    lhsT=w4w[:, 1024 * a + 256 * m : 1024 * a + 256 * m + 256].bitcast(FP4X4),
                    lhsT_scale=w4s[:, 512 * a + 128 * m : 512 * a + 128 * m + 128],
                    rhs=x4w[:, 1024 * a + 2 * t0 : 1024 * a + 2 * (t0 + n)].bitcast(FP4X4),
                    rhs_scale=x4s[:, 512 * a + t0 : 512 * a + t0 + n],
                    start=(a == 0),
                    stop=False,
                )

        def interleave(copy, dst, c0, src, s0, n):
            copy(
                dst[:, 4 * c0 : 4 * (c0 + n)].rearrange("p (c i t) -> p c t i", i=4, t=4),
                src[:, :, s0 : s0 + n].rearrange("p t (c i) -> p c t i", i=4),
            )

        x_codes = keep.tile([P, T], U32, align_bytes=64, name="x_codes")
        x_planes = keep.tile([P, T], U8, align_bytes=64, name="x_planes")
        xg = [keep.tile([P, 1024], BF16, align_bytes=64, name="xg%d" % h) for h in range(2)]
        interleave(nc.vector.tensor_copy, xg[0], 0, x_raw, 0, 256)
        interleave(nc.scalar.copy, xg[1], 64, x_raw, 320, 192)
        interleave(nc.vector.tensor_copy, xg[1], 0, x_raw, 256, 64)
        for h in range(2):
            cols = slice(256 * h, 256 * h + 256)
            nc.vector.quantize_mx(out=x_codes[:, cols].bitcast(FP8X4), scales=x_planes[:, cols], in_=xg[h][:])

        w_codes = keep.tile([P, M], U32, align_bytes=64, name="w_codes")
        w_planes = keep.tile([P, M], U8, align_bytes=64, name="w_planes")
        res = [keep.tile([P, T], F32, name="res%d" % m) for m in range(4)]
        for h in range(2):
            wg = [keep.tile([P, 512], BF16, align_bytes=64, name="wg%d_%d" % (h, i)) for i in range(2)]
            interleave(nc.vector.tensor_copy, wg[0], 0, w_raw[h], 0, 128)
            interleave(nc.scalar.copy, wg[1], 32, w_raw[h], 160, 96)
            interleave(nc.vector.tensor_copy, wg[1], 0, w_raw[h], 128, 32)
            for i in range(2):
                cols = slice(256 * h + 128 * i, 256 * h + 128 * i + 128)
                nc.vector.quantize_mx(out=w_codes[:, cols].bitcast(FP8X4), scales=w_planes[:, cols], in_=wg[i][:])
            for m in (2 * h, 2 * h + 1):
                cols = slice(128 * m, 128 * m + 128)
                for t0 in ((0,) if h == 0 else (0, 256)):
                    bank, n = acc[m, t0]
                    nc.tensor.matmul_mx(
                        out=bank[:],
                        lhsT=w_codes[:, cols].bitcast(FP8X4),
                        lhsT_scale=w_planes[:, cols],
                        rhs=x_codes[:, t0 : t0 + n].bitcast(FP8X4),
                        rhs_scale=x_planes[:, t0 : t0 + n],
                        start=False,
                        stop=True,
                    )
        nc.scalar.copy(res[0][:], acc[0, 0][0][:])
        nc.sync.dma_start(out=out[0:128, :], in_=res[0][:])
        nc.vector.tensor_copy(res[1][:], acc[1, 0][0][:])
        nc.sync.dma_start(out=out[128:256, :], in_=res[1][:])
        for m in (2, 3):
            nc.scalar.copy(res[m][:, 0:256], acc[m, 0][0][:])
            nc.vector.tensor_copy(res[m][:, 256:512], acc[m, 256][0][:])
            nc.sync.dma_start(out=out[128 * m : 128 * m + 128, :], in_=res[m][:])
